import numpy as np
import ml_dtypes


def mxq(x, axis, fmt="e4m3"):
    dtype, down = {"e4m3": (ml_dtypes.float8_e4m3fn, 7), "e5m2": (ml_dtypes.float8_e5m2, 14)}[fmt]
    v = np.moveaxis(np.asarray(x, np.float32).astype(ml_dtypes.bfloat16).astype(np.float64), axis, -1)
    blocks = v.reshape(v.shape[:-1] + (-1, 32))
    amax = np.abs(blocks).max(-1, keepdims=True)
    byte = np.maximum(np.where(amax > 0, np.frexp(amax)[1] - 1 + 127, 0) - down, 1)
    scale = np.exp2(byte - 127.0)
    codes = (blocks / scale).astype(np.float32).astype(dtype).astype(np.float64)
    return np.moveaxis((codes * scale).reshape(v.shape), -1, axis)


WIDE = False


def mx_kscale(k, group=512):
    if not WIDE:
        return np.ones(k)
    levels = np.array([18, -18])
    if group != 512:
        return np.exp2(np.random.permutation(np.resize(levels, k // group))).repeat(group)
    if k % 512:
        return np.exp2(np.random.permutation(np.resize(levels, k // 32))).repeat(32)
    a = np.empty((k // 512, 16))
    for p in range(k // 512):
        a[p, :8] = np.random.permutation(np.resize(levels, 8))
        for g in range(8):
            far = levels[np.abs(levels - a[p, g]) >= 10]
            a[p, g + 8] = far[np.random.randint(len(far))]
    return np.exp2(a.ravel()).repeat(32)


def f64(x):
    return np.asarray(x).astype(np.float64)


def softplus(v):
    return np.log(1.0 + np.exp(v))


G, D, M, O, N = 4, 128, 128, 128, 512


def sgn(shape):
    return np.random.uniform(0.5, 2.0, shape) * np.where(np.random.standard_normal(shape) < 0, -1.0, 1.0)


def setup_inputs():
    n = np.random.standard_normal
    s_d = mx_kscale(D, 0)
    s_m = mx_kscale(M, 0)
    return {
        "x": (n((G, D, N)) * s_d[:, None]).astype(np.float32),
        "w1": (n((G, D, M)) / np.sqrt(D) / s_d[:, None]).astype(np.float32),
        "w2": (n((G, D, M)) / np.sqrt(D) / s_d[:, None]).astype(np.float32),
        "re": (np.random.uniform(50.0, 200.0, (G, M, 1))).astype(np.float32),
        "hs": (sgn((G, M, 1)) * s_m[:, None]).astype(np.float32),
        "wo2": (n((G, M, O)) / np.sqrt(M) / s_m[:, None]).astype(np.float32),
        "res": (0.5 * n((G, O, N))).astype(np.float32),
    }


def reference(x, w1, w2, re, hs, wo2, res):
    w1q = mxq(f64(w1), 1, "e4m3")
    xq = mxq(f64(x), 1, "e4m3")
    z1 = w1q.transpose(0, 2, 1) @ xq
    w2q = mxq(f64(w2), 1, "e4m3")
    z2 = w2q.transpose(0, 2, 1) @ xq
    p1 = softplus(z1)
    zs = np.sum(p1, axis=-1, keepdims=True) + f64(re)
    h = p1 / zs * np.tanh(z2) * 512.0
    hh = h * f64(hs)
    wo2q = mxq(f64(wo2), 1, "e4m3")
    hhq = mxq(hh, 1, "e4m3")
    y0 = wo2q.transpose(0, 2, 1) @ hhq
    y = y0 + f64(res)
    return y

@@ -1,0 +1,162 @@
+from contextlib import ExitStack
+
+import concourse.mybir as mybir
+
+G, D, M, O, N = 4, 128, 128, 128, 512
+FLOPS = 2 * G * N * (2 * D * M + M * O)
+
+F32 = mybir.dt.float32
+BF16 = mybir.dt.bfloat16
+U32 = mybir.dt.uint32
+U8 = mybir.dt.uint8
+FP8X4 = mybir.dt.float8_e4m3fn_x4
+ACT = mybir.ActivationFunctionType
+ALU = mybir.AluOpType
+
+P = 128
+PACK = 4
+ROWS = 32
+RUN = 4
+HALF = N // 2
+COLS = 128
+CAP = 32.0
+EXP_CAP = 78962960182680.69
+SPLIT = 176
+
+
+def interleaved_views(dst, src):
+    return (
+        dst.rearrange("p (c i) j -> p c j i", i=RUN),
+        src.rearrange("p j (c i) -> p c j i", i=RUN),
+    )
+
+
+def tile_rows_frowshare_kernel(tc, x, w1, w2, re, hs, wo2, res, out):
+    nc = tc.nc
+    with ExitStack() as ctx:
+        sb = ctx.enter_context(tc.tile_pool(name="sb", bufs=1))
+        ps = ctx.enter_context(tc.psum_pool(name="ps", bufs=1))
+        ctx.enter_context(tc.manual_schedule())
+
+        def packed(t):
+            return t.rearrange("g (p j) c -> (g p) j c", j=PACK)
+
+        def quantize(name, grouped, width):
+            codes = sb.tile([P, width], U32, name=name + "_codes", align_bytes=64)
+            scales = sb.tile([P, width], U8, name=name + "_scales", align_bytes=64)
+            nc.vector.quantize_mx(out=codes[:].bitcast(FP8X4), scales=scales[:], in_=grouped.rearrange("p c j -> p (c j)"))
+            return codes, scales
+
+        def product(bank, g, weights, acts, h):
+            rows = slice(ROWS * g, ROWS * (g + 1))
+            for c in range(0, HALF, COLS):
+                nc.tensor.matmul_mx(
+                    out=bank[:, HALF * h + c:HALF * h + c + COLS],
+                    lhsT=weights[0][rows, :].bitcast(FP8X4),
+                    lhsT_scale=weights[1][rows, :],
+                    rhs=acts[0][rows, c:c + COLS].bitcast(FP8X4),
+                    rhs_scale=acts[1][rows, c:c + COLS],
+                    start=True,
+                    stop=True,
+                )
+
+        halves = [slice(HALF * h, HALF * (h + 1)) for h in range(2)]
+        x_raw = [sb.tile([P, PACK, HALF], F32, name="x_raw_%d" % h) for h in range(2)]
+        w2_raw = sb.tile([P, PACK, M], F32)
+        w1_raw = sb.tile([P, PACK, M], F32)
+        wo_raw = sb.tile([P, PACK, O], F32)
+        hs_sb = sb.tile([P, G], F32)
+        re_sb = sb.tile([P, G], F32)
+        res_sb = sb.tile([P, G, N], F32)
+        nc.sync.dma_start(out=x_raw[0][:], in_=packed(x)[:, :, halves[0]])
+        nc.sync.dma_start(out=w1_raw[:], in_=packed(w1))
+        nc.sync.dma_start(out=x_raw[1][:], in_=packed(x)[:, :, halves[1]])
+        nc.sync.dma_start(out=w2_raw[:], in_=packed(w2))
+        with nc.allow_non_contiguous_dma(reason="one value a partition and group"):
+            nc.sync.dma_start(out=hs_sb[:], in_=hs.rearrange("g m one -> m (g one)"))
+            nc.sync.dma_start(out=re_sb[:], in_=re.rearrange("g m one -> m (g one)"))
+        nc.sync.dma_start(out=wo_raw[:], in_=packed(wo2))
+        nc.sync.dma_start(out=res_sb[:], in_=res.rearrange("g o n -> o g n"))
+
+        x_bf = [sb.tile([P, HALF, PACK], BF16, name="x_bf_%d" % h, align_bytes=64) for h in range(2)]
+        w2_bf = sb.tile([P, M, PACK], BF16, align_bytes=64)
+        w1_bf = sb.tile([P, M, PACK], BF16, align_bytes=64)
+        wo_bf = sb.tile([P, O, PACK], BF16, align_bytes=64)
+        z1 = [ps.tile([P, N], F32, name="z1_%d" % g) for g in range(G)]
+        z2 = [ps.tile([P, N], F32, name="z2_%d" % g) for g in range(G)]
+        th = [sb.tile([P, N], F32, name="th_%d" % g) for g in range(G)]
+        big = [sb.tile([P, N], F32, name="big_%d" % g) for g in range(G)]
+        ex = [sb.tile([P, N], F32, name="ex_%d" % g) for g in range(G)]
+        gate = [sb.tile([P, N], F32, name="gate_%d" % g) for g in range(G)]
+        sp = [sb.tile([P, N], F32, name="sp_%d" % g) for g in range(G)]
+        hh = [sb.tile([P, N], BF16, name="hh_%d" % g) for g in range(G)]
+        big_sum = sb.tile([P, G], F32)
+        sp_sum = sb.tile([P, G], F32)
+        rest = sb.tile([P, G], F32)
+        zs = sb.tile([P, G], F32)
+        inv = sb.tile([P, G], F32)
+        hs16 = sb.tile([P, G], F32)
+
+        nc.vector.tensor_copy(*interleaved_views(x_bf[0][:], x_raw[0][:]))
+        nc.scalar.copy(*interleaved_views(w1_bf[:], w1_raw[:]))
+        xq = [quantize("x0", x_bf[0][:], HALF)]
+        w1q = quantize("w1", w1_bf[:], M)
+        for g in range(G):
+            product(z1[g], g, w1q, xq[0], 0)
+            nc.scalar.activation(out=ex[g][:, halves[0]], in_=z1[g][:, halves[0]], func=ACT.Exp)
+
+        nc.vector.tensor_copy(*interleaved_views(x_bf[1][:], x_raw[1][:]))
+        nc.vector.tensor_copy(*interleaved_views(w2_bf[:], w2_raw[:]))
+        xq.append(quantize("x1", x_bf[1][:], HALF))
+        w2q = quantize("w2", w2_bf[:], M)
+        nc.vector.tensor_scalar(out=hs16[:], in0=hs_sb[:], scalar1=N / CAP, scalar2=None, op0=ALU.mult)
+        for g in range(G):
+            product(z1[g], g, w1q, xq[1], 1)
+            nc.scalar.activation(out=ex[g][:, halves[1]], in_=z1[g][:, halves[1]], func=ACT.Exp)
+            nc.vector.tensor_scalar(out=big[g][:], in0=z1[g][:], scalar1=CAP, scalar2=None, op0=ALU.max, op1=ALU.add,
+                                    accum_out=big_sum[:, g:g + 1])
+        for g in range(G):
+            for h in range(2):
+                product(z2[g], g, w2q, xq[h], h)
+            nc.scalar.activation(out=th[g][:], in_=z2[g][:], func=ACT.Tanh)
+        for g in range(G):
+            nc.vector.tensor_scalar(out=ex[g][:], in0=ex[g][:], scalar1=EXP_CAP, scalar2=None, op0=ALU.min)
+        nc.vector.scalar_tensor_tensor(out=rest[:], in0=big_sum[:], scalar=-CAP * N, in1=re_sb[:], op0=ALU.add, op1=ALU.add)
+        for g in range(G):
+            nc.vector.scalar_tensor_tensor(out=gate[g][:], in0=big[g][:], scalar=hs16[:, g:g + 1], in1=th[g][:],
+                                           op0=ALU.mult, op1=ALU.mult)
+        for g in range(G):
+            nc.scalar.activation(out=sp[g][:], in_=ex[g][:], func=ACT.Ln, bias=1.0, accum_out=sp_sum[:, g:g + 1])
+
+        h_rows = [sb.tile([P, PACK, HALF], BF16, name="h_rows_%d" % h) for h in range(2)]
+
+        def total(g):
+            nc.vector.tensor_tensor(out=zs[:, g:g + 1], in0=sp_sum[:, g:g + 1], in1=rest[:, g:g + 1], op=ALU.add)
+
+        total(0)
+        for g in range(G):
+            nc.vector.reciprocal(out=inv[:, g:g + 1], in_=zs[:, g:g + 1])
+            if g + 1 < G:
+                total(g + 1)
+            pieces = halves if g == G - 1 else [slice(0, N)]
+            for cols in pieces:
+                nc.vector.scalar_tensor_tensor(out=hh[g][:, cols], in0=sp[g][:, cols], scalar=inv[:, g:g + 1],
+                                               in1=gate[g][:, cols], op0=ALU.mult, op1=ALU.mult)
+            for h in range(2):
+                nc.sync.dma_start(out=h_rows[h][ROWS * g:ROWS * (g + 1), :, :], in_=hh[g][:, halves[h]])
+
+        nc.vector.tensor_copy(*interleaved_views(wo_bf[:], wo_raw[:]))
+        woq = quantize("wo", wo_bf[:], O)
+
+        h_bf = [sb.tile([P, HALF, PACK], BF16, name="h_bf_%d" % h, align_bytes=64) for h in range(2)]
+        for h in range(2):
+            nc.vector.tensor_copy(*interleaved_views(h_bf[h][:, :SPLIT, :], h_rows[h][:, :, :SPLIT]))
+            nc.scalar.copy(*interleaved_views(h_bf[h][:, SPLIT:, :], h_rows[h][:, :, SPLIT:]))
+        hq = [quantize("h%d" % h, h_bf[h][:], HALF) for h in range(2)]
+
+        y = [sb.tile([P, N], F32, name="y_%d" % g) for g in range(G)]
+        for g in range(G):
+            for h in range(2):
+                product(z2[g], g, woq, hq[h], h)
+            nc.vector.tensor_tensor(out=y[g][:], in0=z2[g][:], in1=res_sb[:, g, :], op=ALU.add)
+            nc.sync.dma_start(out=out[g], in_=y[g][:])

@@ -22,6 +22,7 @@ COLS = 128
 CAP = 32.0
 EXP_CAP = 78962960182680.69
 SPLIT = 176
+ORDER = (0, 2, 1, 3)
 
 
 def interleaved_views(dst, src):
@@ -47,11 +48,11 @@ def tile_rows_frowshare_kernel(tc, x, w1, w2, re, hs, wo2, res, out):
             nc.vector.quantize_mx(out=codes[:].bitcast(FP8X4), scales=scales[:], in_=grouped.rearrange("p c j -> p (c j)"))
             return codes, scales
 
-        def product(bank, g, weights, acts, h):
+        def product(sums, g, weights, acts):
             rows = slice(ROWS * g, ROWS * (g + 1))
             for c in range(0, HALF, COLS):
                 nc.tensor.matmul_mx(
-                    out=bank[:, HALF * h + c:HALF * h + c + COLS],
+                    out=sums[:, c:c + COLS],
                     lhsT=weights[0][rows, :].bitcast(FP8X4),
                     lhsT_scale=weights[1][rows, :],
                     rhs=acts[0][rows, c:c + COLS].bitcast(FP8X4),
@@ -86,7 +87,7 @@ def tile_rows_frowshare_kernel(tc, x, w1, w2, re, hs, wo2, res, out):
         z2 = [ps.tile([P, N], F32, name="z2_%d" % g) for g in range(G)]
         th = [sb.tile([P, N], F32, name="th_%d" % g) for g in range(G)]
         big = [sb.tile([P, N], F32, name="big_%d" % g) for g in range(G)]
-        ex = [sb.tile([P, N], F32, name="ex_%d" % g) for g in range(G)]
+        ex = sb.tile([P, G, N], F32)
         gate = [sb.tile([P, N], F32, name="gate_%d" % g) for g in range(G)]
         sp = [sb.tile([P, N], F32, name="sp_%d" % g) for g in range(G)]
         hh = [sb.tile([P, N], BF16, name="hh_%d" % g) for g in range(G)]
@@ -95,68 +96,102 @@ def tile_rows_frowshare_kernel(tc, x, w1, w2, re, hs, wo2, res, out):
         rest = sb.tile([P, G], F32)
         zs = sb.tile([P, G], F32)
         inv = sb.tile([P, G], F32)
-        hs16 = sb.tile([P, G], F32)
 
         nc.vector.tensor_copy(*interleaved_views(x_bf[0][:], x_raw[0][:]))
         nc.scalar.copy(*interleaved_views(w1_bf[:], w1_raw[:]))
         xq = [quantize("x0", x_bf[0][:], HALF)]
         w1q = quantize("w1", w1_bf[:], M)
-        for g in range(G):
-            product(z1[g], g, w1q, xq[0], 0)
-            nc.scalar.activation(out=ex[g][:, halves[0]], in_=z1[g][:, halves[0]], func=ACT.Exp)
+        for g in ORDER:
+            product(z1[g][:, halves[0]], g, w1q, xq[0])
+            nc.scalar.activation(out=ex[:, g, halves[0]], in_=z1[g][:, halves[0]], func=ACT.Exp)
 
         nc.vector.tensor_copy(*interleaved_views(x_bf[1][:], x_raw[1][:]))
         nc.vector.tensor_copy(*interleaved_views(w2_bf[:], w2_raw[:]))
         xq.append(quantize("x1", x_bf[1][:], HALF))
         w2q = quantize("w2", w2_bf[:], M)
-        nc.vector.tensor_scalar(out=hs16[:], in0=hs_sb[:], scalar1=N / CAP, scalar2=None, op0=ALU.mult)
-        for g in range(G):
-            product(z1[g], g, w1q, xq[1], 1)
-            nc.scalar.activation(out=ex[g][:, halves[1]], in_=z1[g][:, halves[1]], func=ACT.Exp)
+
+        def clamp(h):
+            nc.vector.tensor_scalar(out=ex[:, :, halves[h]], in0=ex[:, :, halves[h]], scalar1=EXP_CAP, scalar2=None, op0=ALU.min)
+
+        clamp(0)
+        for g in ORDER:
+            product(z1[g][:, halves[1]], g, w1q, xq[1])
+            nc.scalar.activation(out=ex[:, g, halves[1]], in_=z1[g][:, halves[1]], func=ACT.Exp)
             nc.vector.tensor_scalar(out=big[g][:], in0=z1[g][:], scalar1=CAP, scalar2=None, op0=ALU.max, op1=ALU.add,
                                     accum_out=big_sum[:, g:g + 1])
-        for g in range(G):
+        for g in ORDER:
             for h in range(2):
-                product(z2[g], g, w2q, xq[h], h)
+                product(z2[g][:, halves[h]], g, w2q, xq[h])
             nc.scalar.activation(out=th[g][:], in_=z2[g][:], func=ACT.Tanh)
-        for g in range(G):
-            nc.vector.tensor_scalar(out=ex[g][:], in0=ex[g][:], scalar1=EXP_CAP, scalar2=None, op0=ALU.min)
+        clamp(1)
         nc.vector.scalar_tensor_tensor(out=rest[:], in0=big_sum[:], scalar=-CAP * N, in1=re_sb[:], op0=ALU.add, op1=ALU.add)
-        for g in range(G):
-            nc.vector.scalar_tensor_tensor(out=gate[g][:], in0=big[g][:], scalar=hs16[:, g:g + 1], in1=th[g][:],
+        for g in ORDER:
+            nc.vector.scalar_tensor_tensor(out=gate[g][:], in0=big[g][:], scalar=hs_sb[:, g:g + 1], in1=th[g][:],
                                            op0=ALU.mult, op1=ALU.mult)
-        for g in range(G):
-            nc.scalar.activation(out=sp[g][:], in_=ex[g][:], func=ACT.Ln, bias=1.0, accum_out=sp_sum[:, g:g + 1])
+        for g in ORDER:
+            nc.scalar.activation(out=sp[g][:], in_=ex[:, g, :], func=ACT.Ln, bias=1.0, accum_out=sp_sum[:, g:g + 1])
 
         h_rows = [sb.tile([P, PACK, HALF], BF16, name="h_rows_%d" % h) for h in range(2)]
 
         def total(g):
-            nc.vector.tensor_tensor(out=zs[:, g:g + 1], in0=sp_sum[:, g:g + 1], in1=rest[:, g:g + 1], op=ALU.add)
+            nc.vector.tensor_scalar(out=zs[:, g:g + 1], in0=sp_sum[:, g:g + 1], scalar1=rest[:, g:g + 1], scalar2=CAP / N,
+                                    op0=ALU.add, op1=ALU.mult)
 
-        total(0)
-        for g in range(G):
+        def invert(g):
             nc.vector.reciprocal(out=inv[:, g:g + 1], in_=zs[:, g:g + 1])
-            if g + 1 < G:
-                total(g + 1)
-            pieces = halves if g == G - 1 else [slice(0, N)]
-            for cols in pieces:
-                nc.vector.scalar_tensor_tensor(out=hh[g][:, cols], in0=sp[g][:, cols], scalar=inv[:, g:g + 1],
-                                               in1=gate[g][:, cols], op0=ALU.mult, op1=ALU.mult)
-            for h in range(2):
-                nc.sync.dma_start(out=h_rows[h][ROWS * g:ROWS * (g + 1), :, :], in_=hh[g][:, halves[h]])
+
+        def scale(g, cols):
+            nc.vector.scalar_tensor_tensor(out=hh[g][:, cols], in0=sp[g][:, cols], scalar=inv[:, g:g + 1],
+                                           in1=gate[g][:, cols], op0=ALU.mult, op1=ALU.mult)
+
+        def move(g, h):
+            queue = nc.sync if g < G // 2 else nc.scalar
+            queue.dma_start(out=h_rows[h][ROWS * g:ROWS * (g + 1), :, :], in_=hh[g][:, halves[h]])
+
+        first, second, third, fourth = ORDER
+        total(first)
+        invert(first)
+        total(second)
+        scale(first, slice(0, N))
+        invert(second)
+        total(third)
+        scale(second, slice(0, N))
+        invert(third)
+        total(fourth)
+        scale(third, halves[0])
+        invert(fourth)
+        scale(third, halves[1])
+        scale(fourth, halves[0])
+        scale(fourth, halves[1])
+        for g, h in ((first, 0), (first, 1), (second, 0), (third, 0), (fourth, 0), (second, 1), (third, 1), (fourth, 1)):
+            move(g, h)
 
         nc.vector.tensor_copy(*interleaved_views(wo_bf[:], wo_raw[:]))
         woq = quantize("wo", wo_bf[:], O)
 
         h_bf = [sb.tile([P, HALF, PACK], BF16, name="h_bf_%d" % h, align_bytes=64) for h in range(2)]
-        for h in range(2):
-            nc.vector.tensor_copy(*interleaved_views(h_bf[h][:, :SPLIT, :], h_rows[h][:, :, :SPLIT]))
-            nc.scalar.copy(*interleaved_views(h_bf[h][:, SPLIT:, :], h_rows[h][:, :, SPLIT:]))
-        hq = [quantize("h%d" % h, h_bf[h][:], HALF) for h in range(2)]
+        nc.vector.tensor_copy(*interleaved_views(h_bf[0][:, :SPLIT, :], h_rows[0][:, :, :SPLIT]))
+        nc.scalar.copy(*interleaved_views(h_bf[0][:, SPLIT:, :], h_rows[0][:, :, SPLIT:]))
+        nc.scalar.copy(*interleaved_views(h_bf[1][:], h_rows[1][:]))
 
-        y = [sb.tile([P, N], F32, name="y_%d" % g) for g in range(G)]
+        y = [sb.tile([P, G, HALF], F32, name="y_%d" % h) for h in range(2)]
+        out_rows = out.rearrange("g o n -> o g n")
+        banks = (z2, z1)
+
+        def second_layer(h):
+            hq = quantize("h%d" % h, h_bf[h][:], HALF)
+            for g in range(G):
+                product(banks[h][g][:, :HALF], g, woq, hq)
+
+        def residual(g, h):
+            nc.vector.tensor_tensor(out=y[h][:, g, :], in0=banks[h][g][:, :HALF], in1=res_sb[:, g, halves[h]], op=ALU.add)
+
+        second_layer(0)
+        for g in range(G - 1):
+            residual(g, 0)
+        second_layer(1)
+        residual(G - 1, 0)
+        nc.sync.dma_start(out=out_rows[:, :, halves[0]], in_=y[0][:])
         for g in range(G):
-            for h in range(2):
-                product(z2[g], g, woq, hq[h], h)
-            nc.vector.tensor_tensor(out=y[g][:], in0=z2[g][:], in1=res_sb[:, g, :], op=ALU.add)
-            nc.sync.dma_start(out=out[g], in_=y[g][:])
+            residual(g, 1)
+            nc.sync.dma_start(out=out_rows[:, g, halves[1]], in_=y[1][:, g, :])

from contextlib import ExitStack

import concourse.mybir as mybir

G, D, M, O, N = 4, 128, 128, 128, 512
FLOPS = 2 * G * N * (2 * D * M + M * O)

F32 = mybir.dt.float32
BF16 = mybir.dt.bfloat16
U32 = mybir.dt.uint32
U8 = mybir.dt.uint8
FP8X4 = mybir.dt.float8_e4m3fn_x4
ACT = mybir.ActivationFunctionType
ALU = mybir.AluOpType

P = 128
PACK = 4
ROWS = 32
RUN = 4
HALF = N // 2
COLS = 128
CAP = 32.0
EXP_CAP = 78962960182680.69
SPLIT = 176
ORDER = (0, 2, 1, 3)


def interleaved_views(dst, src):
    return (
        dst.rearrange("p (c i) j -> p c j i", i=RUN),
        src.rearrange("p j (c i) -> p c j i", i=RUN),
    )


def tile_rows_frowshare_kernel(tc, x, w1, w2, re, hs, wo2, res, out):
    nc = tc.nc
    with ExitStack() as ctx:
        sb = ctx.enter_context(tc.tile_pool(name="sb", bufs=1))
        ps = ctx.enter_context(tc.psum_pool(name="ps", bufs=1))
        ctx.enter_context(tc.manual_schedule())

        def packed(t):
            return t.rearrange("g (p j) c -> (g p) j c", j=PACK)

        def quantize(name, grouped, width):
            codes = sb.tile([P, width], U32, name=name + "_codes", align_bytes=64)
            scales = sb.tile([P, width], U8, name=name + "_scales", align_bytes=64)
            nc.vector.quantize_mx(out=codes[:].bitcast(FP8X4), scales=scales[:], in_=grouped.rearrange("p c j -> p (c j)"))
            return codes, scales

        def product(sums, g, weights, acts):
            rows = slice(ROWS * g, ROWS * (g + 1))
            for c in range(0, HALF, COLS):
                nc.tensor.matmul_mx(
                    out=sums[:, c:c + COLS],
                    lhsT=weights[0][rows, :].bitcast(FP8X4),
                    lhsT_scale=weights[1][rows, :],
                    rhs=acts[0][rows, c:c + COLS].bitcast(FP8X4),
                    rhs_scale=acts[1][rows, c:c + COLS],
                    start=True,
                    stop=True,
                )

        halves = [slice(HALF * h, HALF * (h + 1)) for h in range(2)]
        x_raw = [sb.tile([P, PACK, HALF], F32, name="x_raw_%d" % h) for h in range(2)]
        w2_raw = sb.tile([P, PACK, M], F32)
        w1_raw = sb.tile([P, PACK, M], F32)
        wo_raw = sb.tile([P, PACK, O], F32)
        hs_sb = sb.tile([P, G], F32)
        re_sb = sb.tile([P, G], F32)
        res_sb = sb.tile([P, G, N], F32)
        nc.sync.dma_start(out=x_raw[0][:], in_=packed(x)[:, :, halves[0]])
        nc.sync.dma_start(out=w1_raw[:], in_=packed(w1))
        nc.sync.dma_start(out=x_raw[1][:], in_=packed(x)[:, :, halves[1]])
        nc.sync.dma_start(out=w2_raw[:], in_=packed(w2))
        with nc.allow_non_contiguous_dma(reason="one value a partition and group"):
            nc.sync.dma_start(out=hs_sb[:], in_=hs.rearrange("g m one -> m (g one)"))
            nc.sync.dma_start(out=re_sb[:], in_=re.rearrange("g m one -> m (g one)"))
        nc.sync.dma_start(out=wo_raw[:], in_=packed(wo2))
        nc.sync.dma_start(out=res_sb[:], in_=res.rearrange("g o n -> o g n"))

        x_bf = [sb.tile([P, HALF, PACK], BF16, name="x_bf_%d" % h, align_bytes=64) for h in range(2)]
        w2_bf = sb.tile([P, M, PACK], BF16, align_bytes=64)
        w1_bf = sb.tile([P, M, PACK], BF16, align_bytes=64)
        wo_bf = sb.tile([P, O, PACK], BF16, align_bytes=64)
        z1 = [ps.tile([P, N], F32, name="z1_%d" % g) for g in range(G)]
        z2 = [ps.tile([P, N], F32, name="z2_%d" % g) for g in range(G)]
        th = [sb.tile([P, N], F32, name="th_%d" % g) for g in range(G)]
        big = [sb.tile([P, N], F32, name="big_%d" % g) for g in range(G)]
        ex = sb.tile([P, G, N], F32)
        gate = [sb.tile([P, N], F32, name="gate_%d" % g) for g in range(G)]
        sp = [sb.tile([P, N], F32, name="sp_%d" % g) for g in range(G)]
        hh = [sb.tile([P, N], BF16, name="hh_%d" % g) for g in range(G)]
        big_sum = sb.tile([P, G], F32)
        sp_sum = sb.tile([P, G], F32)
        rest = sb.tile([P, G], F32)
        zs = sb.tile([P, G], F32)
        inv = sb.tile([P, G], F32)

        nc.vector.tensor_copy(*interleaved_views(x_bf[0][:], x_raw[0][:]))
        nc.scalar.copy(*interleaved_views(w1_bf[:], w1_raw[:]))
        xq = [quantize("x0", x_bf[0][:], HALF)]
        w1q = quantize("w1", w1_bf[:], M)
        for g in ORDER:
            product(z1[g][:, halves[0]], g, w1q, xq[0])
            nc.scalar.activation(out=ex[:, g, halves[0]], in_=z1[g][:, halves[0]], func=ACT.Exp)

        nc.vector.tensor_copy(*interleaved_views(x_bf[1][:], x_raw[1][:]))
        nc.vector.tensor_copy(*interleaved_views(w2_bf[:], w2_raw[:]))
        xq.append(quantize("x1", x_bf[1][:], HALF))
        w2q = quantize("w2", w2_bf[:], M)

        def clamp(h):
            nc.vector.tensor_scalar(out=ex[:, :, halves[h]], in0=ex[:, :, halves[h]], scalar1=EXP_CAP, scalar2=None, op0=ALU.min)

        clamp(0)
        for g in ORDER:
            product(z1[g][:, halves[1]], g, w1q, xq[1])
            nc.scalar.activation(out=ex[:, g, halves[1]], in_=z1[g][:, halves[1]], func=ACT.Exp)
            nc.vector.tensor_scalar(out=big[g][:], in0=z1[g][:], scalar1=CAP, scalar2=None, op0=ALU.max, op1=ALU.add,
                                    accum_out=big_sum[:, g:g + 1])
        for g in ORDER:
            for h in range(2):
                product(z2[g][:, halves[h]], g, w2q, xq[h])
            nc.scalar.activation(out=th[g][:], in_=z2[g][:], func=ACT.Tanh)
        clamp(1)
        nc.vector.scalar_tensor_tensor(out=rest[:], in0=big_sum[:], scalar=-CAP * N, in1=re_sb[:], op0=ALU.add, op1=ALU.add)
        for g in ORDER:
            nc.vector.scalar_tensor_tensor(out=gate[g][:], in0=big[g][:], scalar=hs_sb[:, g:g + 1], in1=th[g][:],
                                           op0=ALU.mult, op1=ALU.mult)
        for g in ORDER:
            nc.scalar.activation(out=sp[g][:], in_=ex[:, g, :], func=ACT.Ln, bias=1.0, accum_out=sp_sum[:, g:g + 1])

        h_rows = [sb.tile([P, PACK, HALF], BF16, name="h_rows_%d" % h) for h in range(2)]

        def total(g):
            nc.vector.tensor_scalar(out=zs[:, g:g + 1], in0=sp_sum[:, g:g + 1], scalar1=rest[:, g:g + 1], scalar2=CAP / N,
                                    op0=ALU.add, op1=ALU.mult)

        def invert(g):
            nc.vector.reciprocal(out=inv[:, g:g + 1], in_=zs[:, g:g + 1])

        def scale(g, cols):
            nc.vector.scalar_tensor_tensor(out=hh[g][:, cols], in0=sp[g][:, cols], scalar=inv[:, g:g + 1],
                                           in1=gate[g][:, cols], op0=ALU.mult, op1=ALU.mult)

        def move(g, h):
            queue = nc.sync if g < G // 2 else nc.scalar
            queue.dma_start(out=h_rows[h][ROWS * g:ROWS * (g + 1), :, :], in_=hh[g][:, halves[h]])

        first, second, third, fourth = ORDER
        total(first)
        invert(first)
        total(second)
        scale(first, slice(0, N))
        invert(second)
        total(third)
        scale(second, slice(0, N))
        invert(third)
        total(fourth)
        scale(third, halves[0])
        invert(fourth)
        scale(third, halves[1])
        scale(fourth, halves[0])
        scale(fourth, halves[1])
        for g, h in ((first, 0), (first, 1), (second, 0), (third, 0), (fourth, 0), (second, 1), (third, 1), (fourth, 1)):
            move(g, h)

        nc.vector.tensor_copy(*interleaved_views(wo_bf[:], wo_raw[:]))
        woq = quantize("wo", wo_bf[:], O)

        h_bf = [sb.tile([P, HALF, PACK], BF16, name="h_bf_%d" % h, align_bytes=64) for h in range(2)]
        nc.vector.tensor_copy(*interleaved_views(h_bf[0][:, :SPLIT, :], h_rows[0][:, :, :SPLIT]))
        nc.scalar.copy(*interleaved_views(h_bf[0][:, SPLIT:, :], h_rows[0][:, :, SPLIT:]))
        nc.scalar.copy(*interleaved_views(h_bf[1][:], h_rows[1][:]))

        y = [sb.tile([P, G, HALF], F32, name="y_%d" % h) for h in range(2)]
        out_rows = out.rearrange("g o n -> o g n")
        banks = (z2, z1)

        def second_layer(h):
            hq = quantize("h%d" % h, h_bf[h][:], HALF)
            for g in range(G):
                product(banks[h][g][:, :HALF], g, woq, hq)

        def residual(g, h):
            nc.vector.tensor_tensor(out=y[h][:, g, :], in0=banks[h][g][:, :HALF], in1=res_sb[:, g, halves[h]], op=ALU.add)

        second_layer(0)
        for g in range(G - 1):
            residual(g, 0)
        second_layer(1)
        residual(G - 1, 0)
        nc.sync.dma_start(out=out_rows[:, :, halves[0]], in_=y[0][:])
        for g in range(G):
            residual(g, 1)
            nc.sync.dma_start(out=out_rows[:, g, halves[1]], in_=y[1][:, g, :])
